import numpy as np
CORES = [5,21,45,77,85,101,109,125,133,141,189,213]
N = 12
R, T = 2048, 64
CAPP = 16
def entries(a): return a.T.reshape(-1)
def pack(v, P): return np.ascontiguousarray(np.asarray(v, np.int32).reshape(-1, P).T)
def lists(rng, how):
    Q = rng.permutation(N * R)[:N * T]
    if how == "hotrank": Q = R * int(rng.integers(N)) + rng.permutation(R)[:N * T]
    if how == "own": Q = np.concatenate([R * r + rng.permutation(R)[:T] for r in range(N)])
    if how == "sorted": Q = np.sort(Q)
    if how == "edge":
        ends = np.concatenate([R * np.arange(N), R * np.arange(N) + R - 1]); rest = np.setdiff1d(rng.permutation(N * R), ends, assume_unique=True)
        Q = rng.permutation(np.concatenate([ends, rng.permutation(rest)[:N * T - 2 * N]]))
    if how in ("uniform", "full", "sorted", "edge"):
        O = np.stack([rng.permutation(np.repeat(rng.permutation(N)[:T // CAPP], CAPP)) if how == "full" else rng.permutation(np.repeat(np.arange(N), CAPP))[:T] for r in range(N)]).reshape(-1); Q = np.zeros(N * T, np.int64)
        for d in range(N):
            m = np.nonzero(O == d)[0]; w = rng.permutation(R)[:len(m)]
            if how == "edge" and len(m) >= 2: w[:2] = [0, R - 1]; w[2:] = 1 + rng.permutation(R - 2)[:len(m) - 2]
            Q[m] = R * d + w
        if how == "sorted": Q = np.sort(Q.reshape(N, T), axis=1).reshape(-1)
    return {"pos": np.stack([pack(q, 16) for q in Q.reshape(N, T)])}
def setup_inputs(rng):
    return dict({"tab": rng.standard_normal((N, 128, R), dtype=np.float32), "new": rng.standard_normal((N, 128, T), dtype=np.float32)}, **lists(rng, "uniform"))
def setup_inputs_edge(rng):
    d = setup_inputs(rng); d.update(lists(rng, "edge"))
    for k in ("tab", "new"): d[k] = (d[k].astype(np.float32) * 1048576.0).astype(d[k].dtype)
    return d
def setup_inputs_full(rng):
    d = setup_inputs(rng); d.update(lists(rng, "full"))
    for k in ("tab", "new"): d[k] = (d[k].astype(np.float32) * (1 / 1024.0)).astype(d[k].dtype)
    return d
def setup_inputs_sorted(rng):
    d = setup_inputs(rng); d.update(lists(rng, "sorted"))
    return d
def check_inputs(x):
    bad = []
    if x["pos"].min() < 0 or x["pos"].max() >= N * R: bad.append("pos out of range")
    if len(np.unique(x["pos"])) != x["pos"].size: bad.append("a place is named twice")
    if max(int(np.bincount(entries(a) // R, minlength=N).max()) for a in x["pos"]) > CAPP: bad.append("more than CAPP entries of a list point into one rank's part")
    return bad
def reference(tab, new, pos):
    A = np.concatenate(list(tab), axis=1)
    for r in range(N): A[:, entries(pos[r])] = new[r]
    return {"y": np.stack([A[:, R * r:R * r + R] for r in range(N)])}

@@ -1,0 +1,196 @@
+from concourse.bass import DstId, RemoteDMATransfer
+from concourse.mybir import AluOpType, AxisListType, ActivationFunctionType
+
+N, R, TN, CAP = 12, 2048, 64, 16
+BLK = CAP + 1
+GRP, NH = 3, 4
+WIN = R + N * CAP
+EARLY = 1024
+NE1, NE2 = 4, 2
+BIG = 256
+
+SCRATCH = {
+    "tabS": ("sbuf", [128, WIN], "float32"),
+    "newS": ("sbuf", [128, TN], "float32"),
+    "cmp": ("sbuf", [128, N * BLK], "float32"),
+    "land": ("sbuf", [128, N * BLK], "float32"),
+    "hbuf": ("sbuf", [128, GRP * BLK], "float32"),
+    "posK": ("sbuf", [128, 4], "int32"),
+    "ints": ("sbuf", [128, 8], "int32"),
+    "fs": ("sbuf", [128, 8], "float32"),
+    "lab": ("sbuf", [128, 2 * N], "float32"),
+    "iq": ("sbuf", [128, 128], "float32"),
+    "LI": ("sbuf", [128, TN], "bfloat16"),
+    "O2": ("sbuf", [128, 2 * N], "bfloat16"),
+    "mask4": ("sbuf", [128, 4], "bfloat16"),
+    "Sel": ("sbuf", [128, 128], "bfloat16"),
+    "rhsA": ("sbuf", [128, 4], "bfloat16"),
+    "l2": ("sbuf", [128, 128], "float32"),
+    "RP": ("sbuf", [128, N], "float32"),
+    "offS": ("sbuf", [128, 4], "uint16"),
+    "offR": ("sbuf", [128, N], "uint16"),
+    "psC": ("psum", [128, 512], "float32"),
+    "psA": ("psum", [128, 512], "float32"),
+    "psB": ("psum", [128, 512], "float32"),
+}
+SEMAPHORES = ["sv", "sa", "sp", "sg", "s_pos", "s_new", "s_t0", "s_t1", "s_own", "s_st", "hsent", "hin", "hout", "arr"]
+
+
+def _engines(mask, first, n):
+    bits = [b for b in range(16) if (mask >> b) & 1]
+    return sum(1 << b for b in bits[first:first + n])
+
+
+def _helpers(c, T, topo):
+    cores = list(T.cores)
+    near = [x for x in range(max(cores) + 64)
+            if x != c and topo.host(x) == topo.host(c) and topo.chip(x) == topo.chip(c) and T.rank_of(x) is None]
+    cap = [x for x in near if all(topo.may_write(x, d) for d in cores if d != c)]
+    cap.sort(key=lambda x: (topo.die(x) != topo.die(c), x))
+    return cap[:NH]
+
+
+def _helper_program(g, core, T, topo, s, m):
+    cores = list(T.cores)
+    dests = [d for d in range(GRP * m, GRP * m + GRP) if d != s]
+    g.wait_ge(T.sem.hin, NE1)
+    tr = []
+    for i, d in enumerate(dests):
+        rid, pid = topo.addr(cores[d], core)
+        o = BLK * (d - GRP * m)
+        tr.append(RemoteDMATransfer(dst_ids=[DstId(rid=rid, pnc=pid)],
+                                    dma_engine_mask=_engines(topo.mask(core, cores[d]), NE2 * i, NE2),
+                                    remote_sem=T.sem.arr, src=T.hbuf[:, o:o + BLK], dst=T.land[:, BLK * s:BLK * s + BLK]))
+    g.remote_dma_fused(tr, local_sem=T.sem.hout)
+    g.wait_ge(T.sem.hout, NE2 * len(dests))
+
+
+def rank_program(g, core, T, topo):
+    cores = list(T.cores)
+    s = T.rank_of(core)
+    if s is None:
+        for r, c in enumerate(cores):
+            if topo.host(c) == topo.host(core) and topo.chip(c) == topo.chip(core):
+                hs = _helpers(c, T, topo)
+                if core in hs:
+                    _helper_program(g, core, T, topo, r, (hs.index(core) - r) % NH)
+        return
+
+    A_, X = AluOpType, AxisListType.X
+    Copy, Ident = ActivationFunctionType.Copy, ActivationFunctionType.Identity
+    sem = T.sem
+    Q = {"v": g.vector, "a": g.scalar, "p": g.tensor, "s": g.sync, "g": g}
+    V, A, P, S = g.vector, g.scalar, g.tensor, g.sync
+    cnt, seen = {}, {}
+
+    def mark(name, inst, n=1):
+        inst.then_inc(sem[name], n)
+        cnt[name] = cnt.get(name, 0) + n
+        return (name, cnt[name])
+
+    def need(q, *hs):
+        for (n, v) in hs:
+            if seen.get((q, n), 0) < v:
+                Q[q].wait_ge(sem[n], v)
+                seen[(q, n)] = v
+
+    rho = s % 2
+    T0 = R + CAP * s
+    K = TN
+    IN = {n: j for j, n in enumerate(["pI", "aI", "bI", "qI", "dI", "lpI"])}
+    FN = {n: j for j, n in enumerate(["aF", "bF", "trc", "dF", "lpT", "slot", "rnk", "w"])}
+
+    def col(n, rows=TN):
+        if n in IN:
+            return T.ints[0:rows, IN[n]:IN[n] + 1]
+        return T.fs[0:rows, FN[n]:FN[n] + 1]
+
+    h_pos = mark("s_pos", S.dma_start(T.posK[0:K, 0:1], T.pos[:, :]), 16)
+    h_new = mark("s_new", A.dma_start(T.newS[:, :], T.new[:, :]), 16)
+    h_t0 = mark("s_t0", A.dma_start(T.tabS[:, 0:EARLY], T.tab[:, 0:EARLY]), 16)
+
+    v_li = mark("sv", V.memset(T.LI[0:K + 1, :], 1.0))
+    v_or = mark("sv", V.memset(T.O2[K:K + 1, N:2 * N], float(-BIG)))
+    v_cm = mark("sv", V.memset(T.cmp[:, :], 0.0))
+    g_pi = mark("sg", g.iota(col("pI", 128), [[1, 1]], 0, 1))
+    g_lab = mark("sg", g.iota(T.lab[0:K, :], [[0, 2], [1, N]], 0, 0, allow_small_or_imprecise_dtypes=True))
+    need("g", v_li)
+    g_l1 = mark("sg", g.affine_select(T.LI[0:K, :], T.LI[0:K, :], [[1, K]], A_.is_ge, 0.0, 0, -1))
+    need("g", g_l1)
+    g_l2 = mark("sg", g.affine_select(T.LI[0:K, :], T.LI[0:K, :], [[1, K]], A_.not_equal, float(BIG), 0, -1))
+    g_or = mark("sg", g.iota(T.O2[K:K + 1, 0:N], [[BLK, N]], (1 - rho) - BIG, 0, allow_small_or_imprecise_dtypes=True))
+    g_iq = mark("sg", g.iota(T.iq[0:K, :], [[0, 8], [1, 16]], 0, 0, allow_small_or_imprecise_dtypes=True))
+    need("v", g_pi)
+    mark("sv", V.tensor_scalar(col("aI"), col("pI"), 3, None, A_.bitwise_and))
+    mark("sv", V.tensor_scalar(col("bI"), col("pI"), 2, None, A_.logical_shift_right))
+    v_q = mark("sv", V.tensor_scalar(col("qI", 128), col("pI", 128), 15, None, A_.bitwise_and))
+    need("v", v_q)
+    mark("sv", V.tensor_copy(col("aF"), col("aI")))
+    v_bf = mark("sv", V.tensor_copy(col("bF"), col("bI")))
+    v_tr = mark("sv", V.tensor_scalar(col("trc", 128), col("qI", 128), float(T0), None, A_.add))
+    need("v", g_iq, v_bf)
+    v_m4 = mark("sv", V.tensor_scalar(T.mask4[0:K, :], T.iq[0:K, 0:4], col("aF"), None, A_.is_equal))
+    v_sel = mark("sv", V.tensor_scalar(T.Sel[0:K, :], T.iq[0:K, :], col("bF"), None, A_.is_equal))
+
+    need("v", h_pos)
+    c_d = mark("sv", V.tensor_scalar(col("dI"), T.posK[0:K, 0:1], 11, None, A_.logical_shift_right))
+    mark("sv", V.tensor_scalar(col("lpI"), T.posK[0:K, 0:1], R - 1, None, A_.bitwise_and))
+    need("v", c_d)
+    c_df = mark("sv", V.tensor_copy(col("dF"), col("dI")))
+    need("v", c_df, g_lab)
+    c_o = mark("sv", V.tensor_scalar(T.O2[0:K, :], T.lab[0:K, :], col("dF"), None, A_.is_equal))
+    c_lt = mark("sv", V.tensor_scalar(col("lpT"), col("lpI"), float(-T0), None, A_.add))
+    need("p", c_o, v_or, g_or, g_l2)
+    p_c = mark("sp", P.matmul(T.psC[0:K, 0:2 * N], T.LI[0:K + 1, 0:K], T.O2[0:K + 1, 0:2 * N], True, True))
+    need("v", p_c)
+    c_s = mark("sv", V.tensor_reduce(col("slot"), T.psC[0:K, 0:N], X, A_.max))
+    c_r = mark("sv", V.tensor_reduce(col("rnk"), T.psC[0:K, N:2 * N], X, A_.max))
+    need("a", c_s, v_m4)
+    a_ra = mark("sa", A.activation(T.rhsA[0:K, :], T.mask4[0:K, :], Copy, scale=col("slot")))
+    need("p", a_ra, v_sel)
+    p_a = mark("sp", P.matmul(T.psA[:, 0:4], T.Sel[0:K, :], T.rhsA[0:K, :], True, True))
+    need("v", c_r)
+    c_l2 = mark("sv", V.tensor_scalar(T.l2[0:K, :], T.iq[0:K, :], col("rnk"), None, A_.is_equal))
+    need("a", c_r, c_lt)
+    a_w = mark("sa", A.activation(col("w"), col("rnk"), Ident, bias=col("lpT"), scale=-1.0))
+    need("a", a_w)
+    a_rp = mark("sa", A.activation(T.RP[0:K, :], T.O2[0:K, 0:N], Copy, scale=col("w")))
+    need("p", c_l2, a_rp)
+    p_b = mark("sp", P.matmul(T.psB[:, 0:N], T.l2[0:K, :], T.RP[0:K, :], True, True))
+    need("v", p_a)
+    c_of = mark("sv", V.tensor_copy(T.offS[:, :], T.psA[:, 0:4]))
+    need("v", c_of, h_new, v_cm)
+    c_sc = mark("sv", V.tensor_copy(T.cmp[:, :].indirect(T.offS[:, 0:4]), T.newS[:, :]))
+    need("v", c_sc, p_b, v_tr)
+    c_pd = mark("sv", V.tensor_scalar(T.cmp[:, CAP * rho::BLK], T.psB[:, 0:N], col("trc", 128), None, A_.add))
+
+    hs = _helpers(core, T, topo)
+    need("g", c_pd)
+    tr = []
+    for m in range(NH):
+        h = hs[(m + s) % NH]
+        rid, pid = topo.addr(h, core)
+        tr.append(RemoteDMATransfer(dst_ids=[DstId(rid=rid, pnc=pid)],
+                                    dma_engine_mask=_engines(topo.mask(core, h), NE1 * m, NE1), remote_sem=sem.hin,
+                                    src=T.cmp[:, GRP * BLK * m:GRP * BLK * (m + 1)], dst=T.hbuf[:, :]))
+    g.remote_dma_fused(tr, local_sem=sem.hsent)
+    h_sent = ("hsent", NE1 * NH)
+
+    need("s", c_pd)
+    h_own = mark("s_own", S.dma_start(T.land[:, BLK * s:BLK * s + BLK], T.cmp[:, BLK * s:BLK * s + BLK]), 16)
+    need("s", h_sent)
+    h_t1 = mark("s_t1", S.dma_start(T.tabS[:, EARLY:R], T.tab[:, EARLY:R]), 16)
+
+    need("v", h_t0, h_t1, h_own, ("arr", NE2 * (N - 1)))
+    mark("sv", V.tensor_copy(T.offR[:, 0::2], T.land[:, 0::2 * BLK]))
+    last = mark("sv", V.tensor_copy(T.offR[:, 1::2], T.land[:, 2 * BLK - 1::2 * BLK]))
+    for t in range(N // 2):
+        need("v", last)
+        o = 2 * BLK * t + 1
+        last = mark("sv", V.tensor_copy(T.tabS[:, :].indirect(T.offR[:, 2 * t:2 * t + 2]), T.land[:, o:o + 2 * CAP]))
+    need("s", last)
+    h_st = mark("s_st", S.dma_start(T.y[:, :], T.tabS[:, 0:R]), 16)
+
+    need("g", h_sent, h_st, h_pos, h_new, h_t0, h_t1, h_own, ("arr", NE2 * (N - 1)))
+    for name in ("sv", "sa", "sp", "sg"):
+        need("g", (name, cnt[name]))

@@ -3,10 +3,9 @@ from concourse.mybir import AluOpType, AxisListType, ActivationFunctionType
 
 N, R, TN, CAP = 12, 2048, 64, 16
 BLK = CAP + 1
-GRP, NH = 3, 4
+NH = 4
 WIN = R + N * CAP
-EARLY = 1024
-NE1, NE2 = 4, 2
+NE1, NE2 = 4, 4
 BIG = 256
 
 SCRATCH = {
@@ -14,7 +13,7 @@ SCRATCH = {
     "newS": ("sbuf", [128, TN], "float32"),
     "cmp": ("sbuf", [128, N * BLK], "float32"),
     "land": ("sbuf", [128, N * BLK], "float32"),
-    "hbuf": ("sbuf", [128, GRP * BLK], "float32"),
+    "hbuf": ("sbuf", [128, 2 * BLK], "float32"),
     "posK": ("sbuf", [128, 4], "int32"),
     "ints": ("sbuf", [128, 8], "int32"),
     "fs": ("sbuf", [128, 8], "float32"),
@@ -28,12 +27,13 @@ SCRATCH = {
     "l2": ("sbuf", [128, 128], "float32"),
     "RP": ("sbuf", [128, N], "float32"),
     "offS": ("sbuf", [128, 4], "uint16"),
-    "offR": ("sbuf", [128, N], "uint16"),
+    "offR": ("sbuf", [128, 2 * N], "uint16"),
     "psC": ("psum", [128, 512], "float32"),
     "psA": ("psum", [128, 512], "float32"),
     "psB": ("psum", [128, 512], "float32"),
 }
-SEMAPHORES = ["sv", "sa", "sp", "sg", "s_pos", "s_new", "s_t0", "s_t1", "s_own", "s_st", "hsent", "hin", "hout", "arr"]
+SEMAPHORES = ["sv", "sa", "sp", "sg", "s_pos", "s_new", "s_t0", "s_own", "s_st", "hsent", "dsent", "hin", "hout",
+              "arrD", "arrX"]
 
 
 def _engines(mask, first, n):
@@ -50,19 +50,48 @@ def _helpers(c, T, topo):
     return cap[:NH]
 
 
-def _helper_program(g, core, T, topo, s, m):
+def _routes(s, T, topo):
     cores = list(T.cores)
-    dests = [d for d in range(GRP * m, GRP * m + GRP) if d != s]
+    direct = [d for d in range(N) if d != s and topo.may_write(cores[s], cores[d])]
+    calls = []
+    for a in range(0, len(direct), 4):
+        part = direct[a:a + 4]
+        n = 8 // len(part) if len(part) in (1, 2, 4) else 2
+        calls.append([(d, n * i, n) for i, d in enumerate(part)])
+    pairs = [t for t in range(N // 2) if any(d != s and d not in direct for d in (2 * t, 2 * t + 1))]
+    return direct, calls, pairs
+
+
+def _helper_program(g, core, T, topo, s, t):
+    cores = list(T.cores)
+    direct = _routes(s, T, topo)[0]
+    dests = [d for d in (2 * t, 2 * t + 1) if d != s and d not in direct]
     g.wait_ge(T.sem.hin, NE1)
     tr = []
     for i, d in enumerate(dests):
         rid, pid = topo.addr(cores[d], core)
-        o = BLK * (d - GRP * m)
+        o = BLK * (d - 2 * t)
         tr.append(RemoteDMATransfer(dst_ids=[DstId(rid=rid, pnc=pid)],
                                     dma_engine_mask=_engines(topo.mask(core, cores[d]), NE2 * i, NE2),
-                                    remote_sem=T.sem.arr, src=T.hbuf[:, o:o + BLK], dst=T.land[:, BLK * s:BLK * s + BLK]))
+                                    remote_sem=T.sem.arrX, src=T.hbuf[:, o:o + BLK], dst=T.land[:, BLK * s:BLK * s + BLK]))
     g.remote_dma_fused(tr, local_sem=T.sem.hout)
     g.wait_ge(T.sem.hout, NE2 * len(dests))
+
+
+def _runs(xs):
+    out, i = [], 0
+    while i < len(xs):
+        j = i + 1
+        if j < len(xs):
+            st = xs[j] - xs[i]
+            while j + 1 < len(xs) and xs[j + 1] - xs[j] == st:
+                j += 1
+            out.append((xs[i], xs[j], st))
+        else:
+            out.append((xs[i], xs[i], 1))
+            j = i
+        i = j + 1
+    return out
 
 
 def rank_program(g, core, T, topo):
@@ -72,8 +101,10 @@ def rank_program(g, core, T, topo):
         for r, c in enumerate(cores):
             if topo.host(c) == topo.host(core) and topo.chip(c) == topo.chip(core):
                 hs = _helpers(c, T, topo)
-                if core in hs:
-                    _helper_program(g, core, T, topo, r, (hs.index(core) - r) % NH)
+                pairs = _routes(r, T, topo)[2]
+                for i, t in enumerate(pairs):
+                    if hs[(i + r) % NH] == core:
+                        _helper_program(g, core, T, topo, r, t)
         return
 
     A_, X = AluOpType, AxisListType.X
@@ -88,8 +119,8 @@ def rank_program(g, core, T, topo):
         cnt[name] = cnt.get(name, 0) + n
         return (name, cnt[name])
 
-    def need(q, *hs):
-        for (n, v) in hs:
+    def need(q, *hs_):
+        for (n, v) in hs_:
             if seen.get((q, n), 0) < v:
                 Q[q].wait_ge(sem[n], v)
                 seen[(q, n)] = v
@@ -107,7 +138,7 @@ def rank_program(g, core, T, topo):
 
     h_pos = mark("s_pos", S.dma_start(T.posK[0:K, 0:1], T.pos[:, :]), 16)
     h_new = mark("s_new", A.dma_start(T.newS[:, :], T.new[:, :]), 16)
-    h_t0 = mark("s_t0", A.dma_start(T.tabS[:, 0:EARLY], T.tab[:, 0:EARLY]), 16)
+    h_t0 = mark("s_t0", A.dma_start(T.tabS[:, 0:R], T.tab[:, :]), 16)
 
     v_li = mark("sv", V.memset(T.LI[0:K + 1, :], 1.0))
     v_or = mark("sv", V.memset(T.O2[K:K + 1, N:2 * N], float(-BIG)))
@@ -165,32 +196,72 @@ def rank_program(g, core, T, topo):
     c_pd = mark("sv", V.tensor_scalar(T.cmp[:, CAP * rho::BLK], T.psB[:, 0:N], col("trc", 128), None, A_.add))
 
     hs = _helpers(core, T, topo)
+    direct, calls, pairs = _routes(s, T, topo)
     need("g", c_pd)
     tr = []
-    for m in range(NH):
-        h = hs[(m + s) % NH]
+    for i, t in enumerate(pairs):
+        h = hs[(i + s) % NH]
         rid, pid = topo.addr(h, core)
         tr.append(RemoteDMATransfer(dst_ids=[DstId(rid=rid, pnc=pid)],
-                                    dma_engine_mask=_engines(topo.mask(core, h), NE1 * m, NE1), remote_sem=sem.hin,
-                                    src=T.cmp[:, GRP * BLK * m:GRP * BLK * (m + 1)], dst=T.hbuf[:, :]))
+                                    dma_engine_mask=_engines(topo.mask(core, h), NE1 * i, NE1), remote_sem=sem.hin,
+                                    src=T.cmp[:, 2 * BLK * t:2 * BLK * (t + 1)], dst=T.hbuf[:, :]))
     g.remote_dma_fused(tr, local_sem=sem.hsent)
-    h_sent = ("hsent", NE1 * NH)
+    h_sent = ("hsent", NE1 * len(pairs))
+    nd = 0
+    for call in calls:
+        tr = []
+        for (d, first, n) in call:
+            rid, pid = topo.addr(cores[d], core)
+            tr.append(RemoteDMATransfer(dst_ids=[DstId(rid=rid, pnc=pid)],
+                                        dma_engine_mask=_engines(topo.mask(core, cores[d]), first, n), remote_sem=sem.arrD,
+                                        src=T.cmp[:, BLK * d:BLK * d + BLK], dst=T.land[:, BLK * s:BLK * s + BLK]))
+            nd += n
+        g.remote_dma_fused(tr, local_sem=sem.dsent)
+    h_dsent = ("dsent", nd)
 
     need("s", c_pd)
     h_own = mark("s_own", S.dma_start(T.land[:, BLK * s:BLK * s + BLK], T.cmp[:, BLK * s:BLK * s + BLK]), 16)
-    need("s", h_sent)
-    h_t1 = mark("s_t1", S.dma_start(T.tabS[:, EARLY:R], T.tab[:, EARLY:R]), 16)
 
-    need("v", h_t0, h_t1, h_own, ("arr", NE2 * (N - 1)))
-    mark("sv", V.tensor_copy(T.offR[:, 0::2], T.land[:, 0::2 * BLK]))
-    last = mark("sv", V.tensor_copy(T.offR[:, 1::2], T.land[:, 2 * BLK - 1::2 * BLK]))
-    for t in range(N // 2):
-        need("v", last)
-        o = 2 * BLK * t + 1
-        last = mark("sv", V.tensor_copy(T.tabS[:, :].indirect(T.offR[:, 2 * t:2 * t + 2]), T.land[:, o:o + 2 * CAP]))
+    early, n_d, n_x = [s], 0, 0
+    for x in range(N):
+        if x == s:
+            continue
+        hit = [n for call in _routes(x, T, topo)[1] for (d, first, n) in call if d == s]
+        if hit:
+            early.append(x)
+            n_d += hit[0]
+        else:
+            n_x += NE2
+    early.sort()
+    late = [x for x in range(N) if x not in early]
+    h_arrD, h_arrX = ("arrD", n_d), ("arrX", n_x)
+
+    def absorb(group, last):
+        lone = [x for x in group if x % 2 == 1 and x - 1 not in group]
+        for f in (0, 1):
+            for (a, b, st) in _runs([x for x in group if x % 2 == f and x not in lone]):
+                pa, pb = BLK * a + CAP * f, BLK * b + CAP * f
+                last = mark("sv", V.tensor_copy(T.offR[:, a:b + 1:st], T.land[:, pa:pb + 1:BLK * st]))
+        for x in lone:
+            last = mark("sv", V.tensor_copy(T.offR[:, N + x - 1:N + x], T.land[:, BLK * x + CAP:BLK * x + CAP + 1]))
+        for t in range(N // 2):
+            mine = [x for x in (2 * t, 2 * t + 1) if x in group]
+            if not mine:
+                continue
+            need("v", last)
+            o = BLK * mine[0] + (1 - mine[0] % 2)
+            c0 = N + mine[0] - 1 if mine[0] in lone else mine[0]
+            last = mark("sv", V.tensor_copy(T.tabS[:, :].indirect(T.offR[:, c0:c0 + len(mine)]),
+                                            T.land[:, o:o + CAP * len(mine)]))
+        return last
+
+    need("v", h_t0, h_own, h_arrD)
+    last = absorb(early, c_pd)
+    need("v", h_arrX)
+    last = absorb(late, last)
     need("s", last)
     h_st = mark("s_st", S.dma_start(T.y[:, :], T.tabS[:, 0:R]), 16)
 
-    need("g", h_sent, h_st, h_pos, h_new, h_t0, h_t1, h_own, ("arr", NE2 * (N - 1)))
+    need("g", h_sent, h_dsent, h_st, h_pos, h_new, h_t0, h_own, h_arrD, h_arrX)
     for name in ("sv", "sa", "sp", "sg"):
         need("g", (name, cnt[name]))

@@ -5,14 +5,14 @@ N, R, TN, CAP = 12, 2048, 64, 16
 BLK = CAP + 1
 NH = 4
 WIN = R + N * CAP
-NE1, NE2 = 4, 4
 BIG = 256
 
 SCRATCH = {
     "tabS": ("sbuf", [128, WIN], "float32"),
     "newS": ("sbuf", [128, TN], "float32"),
     "cmp": ("sbuf", [128, N * BLK], "float32"),
-    "land": ("sbuf", [128, N * BLK], "float32"),
+    "land": ("sbuf", [128, N, BLK], "float32"),
+    "dat": ("sbuf", [128, N * CAP], "float32"),
     "hbuf": ("sbuf", [128, 2 * BLK], "float32"),
     "posK": ("sbuf", [128, 4], "int32"),
     "ints": ("sbuf", [128, 8], "int32"),
@@ -36,9 +36,19 @@ SEMAPHORES = ["sv", "sa", "sp", "sg", "s_pos", "s_new", "s_t0", "s_own", "s_st",
               "arrD", "arrX"]
 
 
+def _bits(mask):
+    return [b for b in range(16) if (mask >> b) & 1]
+
+
 def _engines(mask, first, n):
-    bits = [b for b in range(16) if (mask >> b) & 1]
-    return sum(1 << b for b in bits[first:first + n])
+    return sum(1 << b for b in _bits(mask)[first:first + n])
+
+
+def _pow2(x):
+    n = 1
+    while 2 * n <= x:
+        n *= 2
+    return n
 
 
 def _helpers(c, T, topo):
@@ -52,46 +62,57 @@ def _helpers(c, T, topo):
 
 def _routes(s, T, topo):
     cores = list(T.cores)
-    direct = [d for d in range(N) if d != s and topo.may_write(cores[s], cores[d])]
+    c = cores[s]
+    direct = [d for d in range(N) if d != s and topo.may_write(c, cores[d])]
     calls = []
     for a in range(0, len(direct), 4):
         part = direct[a:a + 4]
-        n = 8 // len(part) if len(part) in (1, 2, 4) else 2
+        n = _pow2(min(len(_bits(topo.mask(c, cores[d]))) for d in part) // len(part))
         calls.append([(d, n * i, n) for i, d in enumerate(part)])
-    pairs = [t for t in range(N // 2) if any(d != s and d not in direct for d in (2 * t, 2 * t + 1))]
-    return direct, calls, pairs
-
-
-def _helper_program(g, core, T, topo, s, t):
-    cores = list(T.cores)
-    direct = _routes(s, T, topo)[0]
-    dests = [d for d in (2 * t, 2 * t + 1) if d != s and d not in direct]
-    g.wait_ge(T.sem.hin, NE1)
-    tr = []
-    for i, d in enumerate(dests):
-        rid, pid = topo.addr(cores[d], core)
-        o = BLK * (d - 2 * t)
-        tr.append(RemoteDMATransfer(dst_ids=[DstId(rid=rid, pnc=pid)],
-                                    dma_engine_mask=_engines(topo.mask(core, cores[d]), NE2 * i, NE2),
-                                    remote_sem=T.sem.arrX, src=T.hbuf[:, o:o + BLK], dst=T.land[:, BLK * s:BLK * s + BLK]))
-    g.remote_dma_fused(tr, local_sem=T.sem.hout)
-    g.wait_ge(T.sem.hout, NE2 * len(dests))
-
-
-def _runs(xs):
-    out, i = [], 0
-    while i < len(xs):
-        j = i + 1
-        if j < len(xs):
-            st = xs[j] - xs[i]
-            while j + 1 < len(xs) and xs[j + 1] - xs[j] == st:
-                j += 1
-            out.append((xs[i], xs[j], st))
+    others = [d for d in range(N) if d != s and d not in direct]
+    groups, i, two = [], 0, max(0, len(others) - NH)
+    while i < len(others):
+        if two > 0 and i + 1 < len(others) and others[i + 1] == others[i] + 1:
+            groups.append(others[i:i + 2])
+            two, i = two - 1, i + 2
         else:
-            out.append((xs[i], xs[i], 1))
-            j = i
-        i = j + 1
-    return out
+            groups.append(others[i:i + 1])
+            i += 1
+    groups.sort(key=lambda q: -len(q))
+    hs = _helpers(c, T, topo)
+    relay = []
+    for w, call in ((2, 0), (1, 1)):
+        part = [(i, q) for i, q in enumerate(groups) if len(q) == w]
+        for j, (i, q) in enumerate(part):
+            h = hs[(i + s) % NH]
+            n1 = _pow2(len(_bits(topo.mask(c, h))) // len(part))
+            n2 = _pow2(min(len(_bits(topo.mask(h, cores[d]))) for d in q) // w)
+            relay.append((h, q, call, n1 * j, n1, n2))
+    return direct, calls, relay
+
+
+def _order(r, T, topo):
+    early = [x for x in range(N) if x == r or r in _routes(x, T, topo)[0]]
+    return early, [x for x in range(N) if x not in early]
+
+
+def _slot(r, x, T, topo):
+    early, late = _order(r, T, topo)
+    return (early + late).index(x)
+
+
+def _helper_program(g, core, T, topo, s, q, n1, n2):
+    cores = list(T.cores)
+    g.wait_ge(T.sem.hin, n1)
+    tr = []
+    for i, d in enumerate(q):
+        rid, pid = topo.addr(cores[d], core)
+        tr.append(RemoteDMATransfer(dst_ids=[DstId(rid=rid, pnc=pid)],
+                                    dma_engine_mask=_engines(topo.mask(core, cores[d]), n2 * i, n2),
+                                    remote_sem=T.sem.arrX, src=T.hbuf[:, BLK * i:BLK * i + BLK],
+                                    dst=T.land[:, _slot(d, s, T, topo), :]))
+    g.remote_dma_fused(tr, local_sem=T.sem.hout)
+    g.wait_ge(T.sem.hout, n2 * len(q))
 
 
 def rank_program(g, core, T, topo):
@@ -100,11 +121,9 @@ def rank_program(g, core, T, topo):
     if s is None:
         for r, c in enumerate(cores):
             if topo.host(c) == topo.host(core) and topo.chip(c) == topo.chip(core):
-                hs = _helpers(c, T, topo)
-                pairs = _routes(r, T, topo)[2]
-                for i, t in enumerate(pairs):
-                    if hs[(i + r) % NH] == core:
-                        _helper_program(g, core, T, topo, r, t)
+                for (h, q, call, first, n1, n2) in _routes(r, T, topo)[2]:
+                    if h == core:
+                        _helper_program(g, core, T, topo, r, q, n1, n2)
         return
 
     A_, X = AluOpType, AxisListType.X
@@ -125,7 +144,6 @@ def rank_program(g, core, T, topo):
                 Q[q].wait_ge(sem[n], v)
                 seen[(q, n)] = v
 
-    rho = s % 2
     T0 = R + CAP * s
     K = TN
     IN = {n: j for j, n in enumerate(["pI", "aI", "bI", "qI", "dI", "lpI"])}
@@ -149,7 +167,7 @@ def rank_program(g, core, T, topo):
     g_l1 = mark("sg", g.affine_select(T.LI[0:K, :], T.LI[0:K, :], [[1, K]], A_.is_ge, 0.0, 0, -1))
     need("g", g_l1)
     g_l2 = mark("sg", g.affine_select(T.LI[0:K, :], T.LI[0:K, :], [[1, K]], A_.not_equal, float(BIG), 0, -1))
-    g_or = mark("sg", g.iota(T.O2[K:K + 1, 0:N], [[BLK, N]], (1 - rho) - BIG, 0, allow_small_or_imprecise_dtypes=True))
+    g_or = mark("sg", g.iota(T.O2[K:K + 1, 0:N], [[BLK, N]], -BIG, 0, allow_small_or_imprecise_dtypes=True))
     g_iq = mark("sg", g.iota(T.iq[0:K, :], [[0, 8], [1, 16]], 0, 0, allow_small_or_imprecise_dtypes=True))
     need("v", g_pi)
     mark("sv", V.tensor_scalar(col("aI"), col("pI"), 3, None, A_.bitwise_and))
@@ -193,20 +211,24 @@ def rank_program(g, core, T, topo):
     need("v", c_of, h_new, v_cm)
     c_sc = mark("sv", V.tensor_copy(T.cmp[:, :].indirect(T.offS[:, 0:4]), T.newS[:, :]))
     need("v", c_sc, p_b, v_tr)
-    c_pd = mark("sv", V.tensor_scalar(T.cmp[:, CAP * rho::BLK], T.psB[:, 0:N], col("trc", 128), None, A_.add))
+    c_pd = mark("sv", V.tensor_scalar(T.cmp[:, CAP::BLK], T.psB[:, 0:N], col("trc", 128), None, A_.add))
 
-    hs = _helpers(core, T, topo)
-    direct, calls, pairs = _routes(s, T, topo)
+    direct, calls, relay = _routes(s, T, topo)
     need("g", c_pd)
-    tr = []
-    for i, t in enumerate(pairs):
-        h = hs[(i + s) % NH]
-        rid, pid = topo.addr(h, core)
-        tr.append(RemoteDMATransfer(dst_ids=[DstId(rid=rid, pnc=pid)],
-                                    dma_engine_mask=_engines(topo.mask(core, h), NE1 * i, NE1), remote_sem=sem.hin,
-                                    src=T.cmp[:, 2 * BLK * t:2 * BLK * (t + 1)], dst=T.hbuf[:, :]))
-    g.remote_dma_fused(tr, local_sem=sem.hsent)
-    h_sent = ("hsent", NE1 * len(pairs))
+    nh = 0
+    for k in sorted(set(call for (h, q, call, first, n1, n2) in relay)):
+        tr = []
+        for (h, q, call, first, n1, n2) in relay:
+            if call != k:
+                continue
+            rid, pid = topo.addr(h, core)
+            w = BLK * len(q)
+            tr.append(RemoteDMATransfer(dst_ids=[DstId(rid=rid, pnc=pid)],
+                                        dma_engine_mask=_engines(topo.mask(core, h), first, n1), remote_sem=sem.hin,
+                                        src=T.cmp[:, BLK * q[0]:BLK * q[0] + w], dst=T.hbuf[:, 0:w]))
+            nh += n1
+        g.remote_dma_fused(tr, local_sem=sem.hsent)
+    h_sent = ("hsent", nh)
     nd = 0
     for call in calls:
         tr = []
@@ -214,51 +236,30 @@ def rank_program(g, core, T, topo):
             rid, pid = topo.addr(cores[d], core)
             tr.append(RemoteDMATransfer(dst_ids=[DstId(rid=rid, pnc=pid)],
                                         dma_engine_mask=_engines(topo.mask(core, cores[d]), first, n), remote_sem=sem.arrD,
-                                        src=T.cmp[:, BLK * d:BLK * d + BLK], dst=T.land[:, BLK * s:BLK * s + BLK]))
+                                        src=T.cmp[:, BLK * d:BLK * d + BLK], dst=T.land[:, _slot(d, s, T, topo), :]))
             nd += n
         g.remote_dma_fused(tr, local_sem=sem.dsent)
     h_dsent = ("dsent", nd)
 
     need("s", c_pd)
-    h_own = mark("s_own", S.dma_start(T.land[:, BLK * s:BLK * s + BLK], T.cmp[:, BLK * s:BLK * s + BLK]), 16)
+    h_own = mark("s_own", S.dma_start(T.land[:, _slot(s, s, T, topo), :], T.cmp[:, BLK * s:BLK * s + BLK]), 16)
 
-    early, n_d, n_x = [s], 0, 0
-    for x in range(N):
-        if x == s:
-            continue
-        hit = [n for call in _routes(x, T, topo)[1] for (d, first, n) in call if d == s]
-        if hit:
-            early.append(x)
-            n_d += hit[0]
-        else:
-            n_x += NE2
-    early.sort()
-    late = [x for x in range(N) if x not in early]
+    early, late = _order(s, T, topo)
+    n_d = sum(n for x in early if x != s for call in _routes(x, T, topo)[1] for (d, first, n) in call if d == s)
+    n_x = sum(n2 for x in late for (h, q, call, first, n1, n2) in _routes(x, T, topo)[2] if s in q)
     h_arrD, h_arrX = ("arrD", n_d), ("arrX", n_x)
 
-    def absorb(group, last):
-        lone = [x for x in group if x % 2 == 1 and x - 1 not in group]
-        for f in (0, 1):
-            for (a, b, st) in _runs([x for x in group if x % 2 == f and x not in lone]):
-                pa, pb = BLK * a + CAP * f, BLK * b + CAP * f
-                last = mark("sv", V.tensor_copy(T.offR[:, a:b + 1:st], T.land[:, pa:pb + 1:BLK * st]))
-        for x in lone:
-            last = mark("sv", V.tensor_copy(T.offR[:, N + x - 1:N + x], T.land[:, BLK * x + CAP:BLK * x + CAP + 1]))
-        for t in range(N // 2):
-            mine = [x for x in (2 * t, 2 * t + 1) if x in group]
-            if not mine:
-                continue
-            need("v", last)
-            o = BLK * mine[0] + (1 - mine[0] % 2)
-            c0 = N + mine[0] - 1 if mine[0] in lone else mine[0]
-            last = mark("sv", V.tensor_copy(T.tabS[:, :].indirect(T.offR[:, c0:c0 + len(mine)]),
-                                            T.land[:, o:o + CAP * len(mine)]))
-        return last
+    def absorb(a, b, o, landed, before):
+        need("a", *landed)
+        cd = mark("sa", A.activation(T.dat[:, CAP * a:CAP * b], T.land[:, a:b, 0:CAP], Copy))
+        need("v", *landed)
+        cp = mark("sv", V.tensor_copy(T.offR[:, o:o + b - a], T.land[:, a:b, CAP]))
+        need("v", cp, cd, before)
+        return mark("sv", V.tensor_copy(T.tabS[:, :].indirect(T.offR[:, o:o + b - a]), T.dat[:, CAP * a:CAP * b]))
 
-    need("v", h_t0, h_own, h_arrD)
-    last = absorb(early, c_pd)
-    need("v", h_arrX)
-    last = absorb(late, last)
+    ne = len(early)
+    last = absorb(0, ne, 0, (h_own, h_arrD), h_t0)
+    last = absorb(ne, N, ne + ne % 2, (h_arrX,), last)
     need("s", last)
     h_st = mark("s_st", S.dma_start(T.y[:, :], T.tabS[:, 0:R]), 16)
 

@@ -17,10 +17,9 @@ SCRATCH = {
     "posK": ("sbuf", [128, 4], "int32"),
     "ints": ("sbuf", [128, 8], "int32"),
     "fs": ("sbuf", [128, 8], "float32"),
-    "lab": ("sbuf", [128, 2 * N], "float32"),
     "iq": ("sbuf", [128, 128], "float32"),
     "LI": ("sbuf", [128, TN], "bfloat16"),
-    "O2": ("sbuf", [128, 2 * N], "bfloat16"),
+    "O2": ("sbuf", [128, 2 * CAP], "bfloat16"),
     "mask4": ("sbuf", [128, 4], "bfloat16"),
     "Sel": ("sbuf", [128, 128], "bfloat16"),
     "rhsA": ("sbuf", [128, 4], "bfloat16"),
@@ -159,16 +158,14 @@ def rank_program(g, core, T, topo):
     h_t0 = mark("s_t0", A.dma_start(T.tabS[:, 0:R], T.tab[:, :]), 16)
 
     v_li = mark("sv", V.memset(T.LI[0:K + 1, :], 1.0))
-    v_or = mark("sv", V.memset(T.O2[K:K + 1, N:2 * N], float(-BIG)))
+    v_or = mark("sv", V.memset(T.O2[K:K + 1, CAP:2 * CAP], float(-BIG)))
     v_cm = mark("sv", V.memset(T.cmp[:, :], 0.0))
     g_pi = mark("sg", g.iota(col("pI", 128), [[1, 1]], 0, 1))
-    g_lab = mark("sg", g.iota(T.lab[0:K, :], [[0, 2], [1, N]], 0, 0, allow_small_or_imprecise_dtypes=True))
+    g_iq = mark("sg", g.iota(T.iq[0:K + 1, :], [[0, 8], [1, 16]], 0, 0, allow_small_or_imprecise_dtypes=True))
     need("g", v_li)
     g_l1 = mark("sg", g.affine_select(T.LI[0:K, :], T.LI[0:K, :], [[1, K]], A_.is_ge, 0.0, 0, -1))
     need("g", g_l1)
     g_l2 = mark("sg", g.affine_select(T.LI[0:K, :], T.LI[0:K, :], [[1, K]], A_.not_equal, float(BIG), 0, -1))
-    g_or = mark("sg", g.iota(T.O2[K:K + 1, 0:N], [[BLK, N]], -BIG, 0, allow_small_or_imprecise_dtypes=True))
-    g_iq = mark("sg", g.iota(T.iq[0:K, :], [[0, 8], [1, 16]], 0, 0, allow_small_or_imprecise_dtypes=True))
     need("v", g_pi)
     mark("sv", V.tensor_scalar(col("aI"), col("pI"), 3, None, A_.bitwise_and))
     mark("sv", V.tensor_scalar(col("bI"), col("pI"), 2, None, A_.logical_shift_right))
@@ -178,22 +175,24 @@ def rank_program(g, core, T, topo):
     v_bf = mark("sv", V.tensor_copy(col("bF"), col("bI")))
     v_tr = mark("sv", V.tensor_scalar(col("trc", 128), col("qI", 128), float(T0), None, A_.add))
     need("v", g_iq, v_bf)
+    v_o1 = mark("sv", V.tensor_scalar(T.O2[K:K + 1, 0:CAP], T.iq[K:K + 1, 0:CAP], float(BLK), float(-BIG), A_.mult, A_.add))
     v_m4 = mark("sv", V.tensor_scalar(T.mask4[0:K, :], T.iq[0:K, 0:4], col("aF"), None, A_.is_equal))
     v_sel = mark("sv", V.tensor_scalar(T.Sel[0:K, :], T.iq[0:K, :], col("bF"), None, A_.is_equal))
 
     need("v", h_pos)
     c_d = mark("sv", V.tensor_scalar(col("dI"), T.posK[0:K, 0:1], 11, None, A_.logical_shift_right))
-    mark("sv", V.tensor_scalar(col("lpI"), T.posK[0:K, 0:1], R - 1, None, A_.bitwise_and))
     need("v", c_d)
     c_df = mark("sv", V.tensor_copy(col("dF"), col("dI")))
-    need("v", c_df, g_lab)
-    c_o = mark("sv", V.tensor_scalar(T.O2[0:K, :], T.lab[0:K, :], col("dF"), None, A_.is_equal))
+    need("v", c_df)
+    c_o = mark("sv", V.tensor_scalar(T.O2[0:K, :], T.iq[0:K, 0:2 * CAP], col("dF"), None, A_.is_equal))
+    c_lp = mark("sv", V.tensor_scalar(col("lpI"), T.posK[0:K, 0:1], R - 1, None, A_.bitwise_and))
+    need("v", c_lp)
     c_lt = mark("sv", V.tensor_scalar(col("lpT"), col("lpI"), float(-T0), None, A_.add))
-    need("p", c_o, v_or, g_or, g_l2)
-    p_c = mark("sp", P.matmul(T.psC[0:K, 0:2 * N], T.LI[0:K + 1, 0:K], T.O2[0:K + 1, 0:2 * N], True, True))
+    need("p", c_o, v_or, v_o1, g_l2)
+    p_c = mark("sp", P.matmul(T.psC[0:K, 0:2 * CAP], T.LI[0:K + 1, 0:K], T.O2[0:K + 1, 0:2 * CAP], True, True))
     need("v", p_c)
     c_s = mark("sv", V.tensor_reduce(col("slot"), T.psC[0:K, 0:N], X, A_.max))
-    c_r = mark("sv", V.tensor_reduce(col("rnk"), T.psC[0:K, N:2 * N], X, A_.max))
+    c_r = mark("sv", V.tensor_reduce(col("rnk"), T.psC[0:K, CAP:CAP + N], X, A_.max))
     need("a", c_s, v_m4)
     a_ra = mark("sa", A.activation(T.rhsA[0:K, :], T.mask4[0:K, :], Copy, scale=col("slot")))
     need("p", a_ra, v_sel)

@@ -6,14 +6,19 @@ BLK = CAP + 1
 NH = 4
 WIN = R + N * CAP
 BIG = 256
+NL = N + 2
 
 SCRATCH = {
     "tabS": ("sbuf", [128, WIN], "float32"),
     "newS": ("sbuf", [128, TN], "float32"),
+    "hnew": ("sbuf", [128, TN], "float32"),
     "cmp": ("sbuf", [128, N * BLK], "float32"),
     "land": ("sbuf", [128, N, BLK], "float32"),
     "dat": ("sbuf", [128, N * CAP], "float32"),
     "hbuf": ("sbuf", [128, 2 * BLK], "float32"),
+    "lst": ("sbuf", [128, NL], "float32"),
+    "hl": ("sbuf", [128, NL], "float32"),
+    "offH": ("sbuf", [128, 4], "uint16"),
     "posK": ("sbuf", [128, 4], "int32"),
     "ints": ("sbuf", [128, 8], "int32"),
     "fs": ("sbuf", [128, 8], "float32"),
@@ -24,7 +29,7 @@ SCRATCH = {
     "Sel": ("sbuf", [128, 128], "bfloat16"),
     "rhsA": ("sbuf", [128, 4], "bfloat16"),
     "l2": ("sbuf", [128, 128], "float32"),
-    "RP": ("sbuf", [128, N], "float32"),
+    "RP": ("sbuf", [128, NL], "float32"),
     "offS": ("sbuf", [128, 4], "uint16"),
     "offR": ("sbuf", [128, 2 * N], "uint16"),
     "psC": ("psum", [128, 512], "float32"),
@@ -32,7 +37,8 @@ SCRATCH = {
     "psB": ("psum", [128, 512], "float32"),
 }
 SEMAPHORES = ["sv", "sa", "sp", "sg", "s_pos", "s_new", "s_t0", "s_own", "s_st", "hsent", "dsent", "hin", "hout",
-              "arrD", "arrX"]
+              "arrD", "arrX", "hraw", "rsent"]
+PICK = -1
 
 
 def _bits(mask):
@@ -80,12 +86,14 @@ def _routes(s, T, topo):
     groups.sort(key=lambda q: -len(q))
     hs = _helpers(c, T, topo)
     relay = []
-    for w, call in ((2, 0), (1, 1)):
-        part = [(i, q) for i, q in enumerate(groups) if len(q) == w]
+    classes = ((PICK, [(0, groups[0])]),
+               (0, [(i, q) for i, q in enumerate(groups) if len(q) == 2 and i != 0]),
+               (1, [(i, q) for i, q in enumerate(groups) if len(q) == 1]))
+    for call, part in classes:
         for j, (i, q) in enumerate(part):
             h = hs[(i + s) % NH]
             n1 = _pow2(len(_bits(topo.mask(c, h))) // len(part))
-            n2 = _pow2(min(len(_bits(topo.mask(h, cores[d]))) for d in q) // w)
+            n2 = _pow2(min(len(_bits(topo.mask(h, cores[d]))) for d in q) // len(q))
             relay.append((h, q, call, n1 * j, n1, n2))
     return direct, calls, relay
 
@@ -100,18 +108,35 @@ def _slot(r, x, T, topo):
     return (early + late).index(x)
 
 
-def _helper_program(g, core, T, topo, s, q, n1, n2):
+def _helper_program(g, core, T, topo, s, q, call, n1, n2):
     cores = list(T.cores)
-    g.wait_ge(T.sem.hin, n1)
+    sem = T.sem
+    g.wait_ge(sem.hin, n1)
+    if call == PICK:
+        V, A = g.vector, g.scalar
+        Copy = ActivationFunctionType.Copy
+        V.wait_ge(sem.hin, n1)
+        V.tensor_copy(T.offH[:, 0:4:2], T.hl[:, N:N + 2]).then_inc(sem.sv, 1)
+        A.wait_ge(sem.hin, n1)
+        A.activation(T.hbuf[:, CAP::BLK], T.hl[:, q[0]:q[0] + 2], Copy).then_inc(sem.sa, 1)
+        V.wait_ge(sem.sv, 1)
+        V.wait_ge(sem.hraw, n1)
+        V.tensor_copy(T.hbuf[:, 0:CAP], T.hnew[:, :].indirect(T.offH[:, 0:1])).then_inc(sem.sv, 1)
+        A.wait_ge(sem.sv, 1)
+        A.wait_ge(sem.hraw, n1)
+        A.activation(T.hbuf[:, BLK:BLK + CAP], T.hnew[:, :].indirect(T.offH[:, 2:3]), Copy).then_inc(sem.sa, 1)
+        g.wait_ge(sem.hraw, n1)
+        g.wait_ge(sem.sv, 2)
+        g.wait_ge(sem.sa, 2)
     tr = []
     for i, d in enumerate(q):
         rid, pid = topo.addr(cores[d], core)
         tr.append(RemoteDMATransfer(dst_ids=[DstId(rid=rid, pnc=pid)],
                                     dma_engine_mask=_engines(topo.mask(core, cores[d]), n2 * i, n2),
-                                    remote_sem=T.sem.arrX, src=T.hbuf[:, BLK * i:BLK * i + BLK],
+                                    remote_sem=sem.arrX, src=T.hbuf[:, BLK * i:BLK * i + BLK],
                                     dst=T.land[:, _slot(d, s, T, topo), :]))
-    g.remote_dma_fused(tr, local_sem=T.sem.hout)
-    g.wait_ge(T.sem.hout, n2 * len(q))
+    g.remote_dma_fused(tr, local_sem=sem.hout)
+    g.wait_ge(sem.hout, n2 * len(q))
 
 
 def rank_program(g, core, T, topo):
@@ -122,7 +147,7 @@ def rank_program(g, core, T, topo):
             if topo.host(c) == topo.host(core) and topo.chip(c) == topo.chip(core):
                 for (h, q, call, first, n1, n2) in _routes(r, T, topo)[2]:
                     if h == core:
-                        _helper_program(g, core, T, topo, r, q, n1, n2)
+                        _helper_program(g, core, T, topo, r, q, call, n1, n2)
         return
 
     A_, X = AluOpType, AxisListType.X
@@ -145,13 +170,16 @@ def rank_program(g, core, T, topo):
 
     T0 = R + CAP * s
     K = TN
-    IN = {n: j for j, n in enumerate(["pI", "aI", "bI", "qI", "dI", "lpI"])}
-    FN = {n: j for j, n in enumerate(["aF", "bF", "trc", "dF", "lpT", "slot", "rnk", "w"])}
+    IN = {n: j for j, n in enumerate(["pI", "aI", "bI", "dI", "lpI"])}
+    FN = {n: j for j, n in enumerate(["aF", "bF", "jF", "dF", "lpT", "slot", "rnk", "w"])}
 
     def col(n, rows=TN):
         if n in IN:
             return T.ints[0:rows, IN[n]:IN[n] + 1]
         return T.fs[0:rows, FN[n]:FN[n] + 1]
+
+    direct, calls, relay = _routes(s, T, topo)
+    (hp, qp, _c, _f, np1, _n2) = relay[0]
 
     h_pos = mark("s_pos", S.dma_start(T.posK[0:K, 0:1], T.pos[:, :]), 16)
     h_new = mark("s_new", A.dma_start(T.newS[:, :], T.new[:, :]), 16)
@@ -160,24 +188,33 @@ def rank_program(g, core, T, topo):
     v_li = mark("sv", V.memset(T.LI[0:K + 1, :], 1.0))
     v_or = mark("sv", V.memset(T.O2[K:K + 1, CAP:2 * CAP], float(-BIG)))
     v_cm = mark("sv", V.memset(T.cmp[:, :], 0.0))
+    mark("sv", V.memset(T.RP[K:K + 1, 0:N], 1.0))
+    v_rk = mark("sv", V.memset(T.RP[K:K + 1, N:NL], 0.0))
     g_pi = mark("sg", g.iota(col("pI", 128), [[1, 1]], 0, 1))
     g_iq = mark("sg", g.iota(T.iq[0:K + 1, :], [[0, 8], [1, 16]], 0, 0, allow_small_or_imprecise_dtypes=True))
     need("g", v_li)
     g_l1 = mark("sg", g.affine_select(T.LI[0:K, :], T.LI[0:K, :], [[1, K]], A_.is_ge, 0.0, 0, -1))
     need("g", g_l1)
     g_l2 = mark("sg", g.affine_select(T.LI[0:K, :], T.LI[0:K, :], [[1, K]], A_.not_equal, float(BIG), 0, -1))
+
+    need("g", h_new)
+    ridp, pidp = topo.addr(hp, core)
+    mp = _engines(topo.mask(core, hp), 0, np1)
+    g.remote_dma(T.hnew[:, :], T.newS[:, :], sem.hraw, sem.rsent, pidp, ridp, mp)
+    h_rsent = ("rsent", np1)
+
     need("v", g_pi)
     mark("sv", V.tensor_scalar(col("aI"), col("pI"), 3, None, A_.bitwise_and))
-    mark("sv", V.tensor_scalar(col("bI"), col("pI"), 2, None, A_.logical_shift_right))
-    v_q = mark("sv", V.tensor_scalar(col("qI", 128), col("pI", 128), 15, None, A_.bitwise_and))
-    need("v", v_q)
+    v_b = mark("sv", V.tensor_scalar(col("bI"), col("pI"), 2, None, A_.logical_shift_right))
+    need("v", v_b)
     mark("sv", V.tensor_copy(col("aF"), col("aI")))
     v_bf = mark("sv", V.tensor_copy(col("bF"), col("bI")))
-    v_tr = mark("sv", V.tensor_scalar(col("trc", 128), col("qI", 128), float(T0), None, A_.add))
     need("v", g_iq, v_bf)
+    v_jf = mark("sv", V.tensor_scalar(col("jF"), col("aF"), float(CAP), col("bF"), A_.mult, A_.add))
     v_o1 = mark("sv", V.tensor_scalar(T.O2[K:K + 1, 0:CAP], T.iq[K:K + 1, 0:CAP], float(BLK), float(-BIG), A_.mult, A_.add))
     v_m4 = mark("sv", V.tensor_scalar(T.mask4[0:K, :], T.iq[0:K, 0:4], col("aF"), None, A_.is_equal))
     v_sel = mark("sv", V.tensor_scalar(T.Sel[0:K, :], T.iq[0:K, :], col("bF"), None, A_.is_equal))
+    v_lk = mark("sv", V.tensor_scalar(T.l2[K:K + 1, :], T.iq[K:K + 1, :], float(T0), None, A_.add))
 
     need("v", h_pos)
     c_d = mark("sv", V.tensor_scalar(col("dI"), T.posK[0:K, 0:1], 11, None, A_.logical_shift_right))
@@ -188,6 +225,8 @@ def rank_program(g, core, T, topo):
     c_lp = mark("sv", V.tensor_scalar(col("lpI"), T.posK[0:K, 0:1], R - 1, None, A_.bitwise_and))
     need("v", c_lp)
     c_lt = mark("sv", V.tensor_scalar(col("lpT"), col("lpI"), float(-T0), None, A_.add))
+    need("a", c_o, v_jf)
+    a_r2 = mark("sa", A.activation(T.RP[0:K, N:NL], T.O2[0:K, qp[0]:qp[0] + 2], Copy, scale=col("jF")))
     need("p", c_o, v_or, v_o1, g_l2)
     p_c = mark("sp", P.matmul(T.psC[0:K, 0:2 * CAP], T.LI[0:K + 1, 0:K], T.O2[0:K + 1, 0:2 * CAP], True, True))
     need("v", p_c)
@@ -202,20 +241,23 @@ def rank_program(g, core, T, topo):
     need("a", c_r, c_lt)
     a_w = mark("sa", A.activation(col("w"), col("rnk"), Ident, bias=col("lpT"), scale=-1.0))
     need("a", a_w)
-    a_rp = mark("sa", A.activation(T.RP[0:K, :], T.O2[0:K, 0:N], Copy, scale=col("w")))
-    need("p", c_l2, a_rp)
-    p_b = mark("sp", P.matmul(T.psB[:, 0:N], T.l2[0:K, :], T.RP[0:K, :], True, True))
+    a_rp = mark("sa", A.activation(T.RP[0:K, 0:N], T.O2[0:K, 0:N], Copy, scale=col("w")))
+    need("p", c_l2, a_rp, a_r2, v_rk, v_lk)
+    p_b = mark("sp", P.matmul(T.psB[:, 0:NL], T.l2[0:K + 1, :], T.RP[0:K + 1, :], True, True))
+    need("a", p_b)
+    a_ls = mark("sa", A.activation(T.lst[:, :], T.psB[:, 0:NL], Copy))
     need("v", p_a)
     c_of = mark("sv", V.tensor_copy(T.offS[:, :], T.psA[:, 0:4]))
     need("v", c_of, h_new, v_cm)
     c_sc = mark("sv", V.tensor_copy(T.cmp[:, :].indirect(T.offS[:, 0:4]), T.newS[:, :]))
-    need("v", c_sc, p_b, v_tr)
-    c_pd = mark("sv", V.tensor_scalar(T.cmp[:, CAP::BLK], T.psB[:, 0:N], col("trc", 128), None, A_.add))
+    need("v", c_sc, a_ls)
+    c_pd = mark("sv", V.tensor_copy(T.cmp[:, CAP::BLK], T.lst[:, 0:N]))
 
-    direct, calls, relay = _routes(s, T, topo)
+    need("g", a_ls)
+    g.remote_dma(T.hl[:, :], T.lst[:, :], sem.hin, sem.hsent, pidp, ridp, mp)
+    nh = np1
     need("g", c_pd)
-    nh = 0
-    for k in sorted(set(call for (h, q, call, first, n1, n2) in relay)):
+    for k in sorted(set(call for (h, q, call, first, n1, n2) in relay if call != PICK)):
         tr = []
         for (h, q, call, first, n1, n2) in relay:
             if call != k:
@@ -262,6 +304,6 @@ def rank_program(g, core, T, topo):
     need("s", last)
     h_st = mark("s_st", S.dma_start(T.y[:, :], T.tabS[:, 0:R]), 16)
 
-    need("g", h_sent, h_dsent, h_st, h_pos, h_new, h_t0, h_own, h_arrD, h_arrX)
+    need("g", h_sent, h_dsent, h_rsent, h_st, h_pos, h_new, h_t0, h_own, h_arrD, h_arrX)
     for name in ("sv", "sa", "sp", "sg"):
         need("g", (name, cnt[name]))

from concourse.bass import DstId, RemoteDMATransfer
from concourse.mybir import AluOpType, AxisListType, ActivationFunctionType

N, R, TN, CAP = 12, 2048, 64, 16
BLK = CAP + 1
NH = 4
WIN = R + N * CAP
BIG = 256
NL = N + 2

SCRATCH = {
    "tabS": ("sbuf", [128, WIN], "float32"),
    "newS": ("sbuf", [128, TN], "float32"),
    "hnew": ("sbuf", [128, TN], "float32"),
    "cmp": ("sbuf", [128, N * BLK], "float32"),
    "land": ("sbuf", [128, N, BLK], "float32"),
    "dat": ("sbuf", [128, N * CAP], "float32"),
    "hbuf": ("sbuf", [128, 2 * BLK], "float32"),
    "lst": ("sbuf", [128, NL], "float32"),
    "hl": ("sbuf", [128, NL], "float32"),
    "offH": ("sbuf", [128, 4], "uint16"),
    "posK": ("sbuf", [128, 4], "int32"),
    "ints": ("sbuf", [128, 8], "int32"),
    "fs": ("sbuf", [128, 8], "float32"),
    "iq": ("sbuf", [128, 128], "float32"),
    "LI": ("sbuf", [128, TN], "bfloat16"),
    "O2": ("sbuf", [128, 2 * CAP], "bfloat16"),
    "mask4": ("sbuf", [128, 4], "bfloat16"),
    "Sel": ("sbuf", [128, 128], "bfloat16"),
    "rhsA": ("sbuf", [128, 4], "bfloat16"),
    "l2": ("sbuf", [128, 128], "float32"),
    "RP": ("sbuf", [128, NL], "float32"),
    "offS": ("sbuf", [128, 4], "uint16"),
    "offR": ("sbuf", [128, 2 * N], "uint16"),
    "psC": ("psum", [128, 512], "float32"),
    "psA": ("psum", [128, 512], "float32"),
    "psB": ("psum", [128, 512], "float32"),
}
SEMAPHORES = ["sv", "sa", "sp", "sg", "s_pos", "s_new", "s_t0", "s_own", "s_st", "hsent", "dsent", "hin", "hout",
              "arrD", "arrX", "hraw", "rsent"]
PICK = -1


def _bits(mask):
    return [b for b in range(16) if (mask >> b) & 1]


def _engines(mask, first, n):
    return sum(1 << b for b in _bits(mask)[first:first + n])


def _pow2(x):
    n = 1
    while 2 * n <= x:
        n *= 2
    return n


def _helpers(c, T, topo):
    cores = list(T.cores)
    near = [x for x in range(max(cores) + 64)
            if x != c and topo.host(x) == topo.host(c) and topo.chip(x) == topo.chip(c) and T.rank_of(x) is None]
    cap = [x for x in near if all(topo.may_write(x, d) for d in cores if d != c)]
    cap.sort(key=lambda x: (topo.die(x) != topo.die(c), x))
    return cap[:NH]


def _routes(s, T, topo):
    cores = list(T.cores)
    c = cores[s]
    direct = [d for d in range(N) if d != s and topo.may_write(c, cores[d])]
    calls = []
    for a in range(0, len(direct), 4):
        part = direct[a:a + 4]
        n = _pow2(min(len(_bits(topo.mask(c, cores[d]))) for d in part) // len(part))
        calls.append([(d, n * i, n) for i, d in enumerate(part)])
    others = [d for d in range(N) if d != s and d not in direct]
    groups, i, two = [], 0, max(0, len(others) - NH)
    while i < len(others):
        if two > 0 and i + 1 < len(others) and others[i + 1] == others[i] + 1:
            groups.append(others[i:i + 2])
            two, i = two - 1, i + 2
        else:
            groups.append(others[i:i + 1])
            i += 1
    groups.sort(key=lambda q: -len(q))
    hs = _helpers(c, T, topo)
    relay = []
    classes = ((PICK, [(0, groups[0])]),
               (0, [(i, q) for i, q in enumerate(groups) if len(q) == 2 and i != 0]),
               (1, [(i, q) for i, q in enumerate(groups) if len(q) == 1]))
    for call, part in classes:
        for j, (i, q) in enumerate(part):
            h = hs[(i + s) % NH]
            n1 = _pow2(len(_bits(topo.mask(c, h))) // len(part))
            n2 = _pow2(min(len(_bits(topo.mask(h, cores[d]))) for d in q) // len(q))
            relay.append((h, q, call, n1 * j, n1, n2))
    return direct, calls, relay


def _order(r, T, topo):
    early = [x for x in range(N) if x == r or r in _routes(x, T, topo)[0]]
    return early, [x for x in range(N) if x not in early]


def _slot(r, x, T, topo):
    early, late = _order(r, T, topo)
    return (early + late).index(x)


def _helper_program(g, core, T, topo, s, q, call, n1, n2):
    cores = list(T.cores)
    sem = T.sem
    g.wait_ge(sem.hin, n1)
    if call == PICK:
        V, A = g.vector, g.scalar
        Copy = ActivationFunctionType.Copy
        V.wait_ge(sem.hin, n1)
        V.tensor_copy(T.offH[:, 0:4:2], T.hl[:, N:N + 2]).then_inc(sem.sv, 1)
        A.wait_ge(sem.hin, n1)
        A.activation(T.hbuf[:, CAP::BLK], T.hl[:, q[0]:q[0] + 2], Copy).then_inc(sem.sa, 1)
        V.wait_ge(sem.sv, 1)
        V.wait_ge(sem.hraw, n1)
        V.tensor_copy(T.hbuf[:, 0:CAP], T.hnew[:, :].indirect(T.offH[:, 0:1])).then_inc(sem.sv, 1)
        A.wait_ge(sem.sv, 1)
        A.wait_ge(sem.hraw, n1)
        A.activation(T.hbuf[:, BLK:BLK + CAP], T.hnew[:, :].indirect(T.offH[:, 2:3]), Copy).then_inc(sem.sa, 1)
        g.wait_ge(sem.hraw, n1)
        g.wait_ge(sem.sv, 2)
        g.wait_ge(sem.sa, 2)
    tr = []
    for i, d in enumerate(q):
        rid, pid = topo.addr(cores[d], core)
        tr.append(RemoteDMATransfer(dst_ids=[DstId(rid=rid, pnc=pid)],
                                    dma_engine_mask=_engines(topo.mask(core, cores[d]), n2 * i, n2),
                                    remote_sem=sem.arrX, src=T.hbuf[:, BLK * i:BLK * i + BLK],
                                    dst=T.land[:, _slot(d, s, T, topo), :]))
    g.remote_dma_fused(tr, local_sem=sem.hout)
    g.wait_ge(sem.hout, n2 * len(q))


def rank_program(g, core, T, topo):
    cores = list(T.cores)
    s = T.rank_of(core)
    if s is None:
        for r, c in enumerate(cores):
            if topo.host(c) == topo.host(core) and topo.chip(c) == topo.chip(core):
                for (h, q, call, first, n1, n2) in _routes(r, T, topo)[2]:
                    if h == core:
                        _helper_program(g, core, T, topo, r, q, call, n1, n2)
        return

    A_, X = AluOpType, AxisListType.X
    Copy, Ident = ActivationFunctionType.Copy, ActivationFunctionType.Identity
    sem = T.sem
    Q = {"v": g.vector, "a": g.scalar, "p": g.tensor, "s": g.sync, "g": g}
    V, A, P, S = g.vector, g.scalar, g.tensor, g.sync
    cnt, seen = {}, {}

    def mark(name, inst, n=1):
        inst.then_inc(sem[name], n)
        cnt[name] = cnt.get(name, 0) + n
        return (name, cnt[name])

    def need(q, *hs_):
        for (n, v) in hs_:
            if seen.get((q, n), 0) < v:
                Q[q].wait_ge(sem[n], v)
                seen[(q, n)] = v

    T0 = R + CAP * s
    K = TN
    IN = {n: j for j, n in enumerate(["pI", "aI", "bI", "dI", "lpI"])}
    FN = {n: j for j, n in enumerate(["aF", "bF", "jF", "dF", "lpT", "slot", "rnk", "w"])}

    def col(n, rows=TN):
        if n in IN:
            return T.ints[0:rows, IN[n]:IN[n] + 1]
        return T.fs[0:rows, FN[n]:FN[n] + 1]

    direct, calls, relay = _routes(s, T, topo)
    (hp, qp, _c, _f, np1, _n2) = relay[0]

    h_pos = mark("s_pos", S.dma_start(T.posK[0:K, 0:1], T.pos[:, :]), 16)
    h_new = mark("s_new", A.dma_start(T.newS[:, :], T.new[:, :]), 16)
    h_t0 = mark("s_t0", A.dma_start(T.tabS[:, 0:R], T.tab[:, :]), 16)

    v_li = mark("sv", V.memset(T.LI[0:K + 1, :], 1.0))
    v_or = mark("sv", V.memset(T.O2[K:K + 1, CAP:2 * CAP], float(-BIG)))
    v_cm = mark("sv", V.memset(T.cmp[:, :], 0.0))
    mark("sv", V.memset(T.RP[K:K + 1, 0:N], 1.0))
    v_rk = mark("sv", V.memset(T.RP[K:K + 1, N:NL], 0.0))
    g_pi = mark("sg", g.iota(col("pI", 128), [[1, 1]], 0, 1))
    g_iq = mark("sg", g.iota(T.iq[0:K + 1, :], [[0, 8], [1, 16]], 0, 0, allow_small_or_imprecise_dtypes=True))
    need("g", v_li)
    g_l1 = mark("sg", g.affine_select(T.LI[0:K, :], T.LI[0:K, :], [[1, K]], A_.is_ge, 0.0, 0, -1))
    need("g", g_l1)
    g_l2 = mark("sg", g.affine_select(T.LI[0:K, :], T.LI[0:K, :], [[1, K]], A_.not_equal, float(BIG), 0, -1))

    need("g", h_new)
    ridp, pidp = topo.addr(hp, core)
    mp = _engines(topo.mask(core, hp), 0, np1)
    g.remote_dma(T.hnew[:, :], T.newS[:, :], sem.hraw, sem.rsent, pidp, ridp, mp)
    h_rsent = ("rsent", np1)

    need("v", g_pi)
    mark("sv", V.tensor_scalar(col("aI"), col("pI"), 3, None, A_.bitwise_and))
    v_b = mark("sv", V.tensor_scalar(col("bI"), col("pI"), 2, None, A_.logical_shift_right))
    need("v", v_b)
    mark("sv", V.tensor_copy(col("aF"), col("aI")))
    v_bf = mark("sv", V.tensor_copy(col("bF"), col("bI")))
    need("v", g_iq, v_bf)
    v_jf = mark("sv", V.tensor_scalar(col("jF"), col("aF"), float(CAP), col("bF"), A_.mult, A_.add))
    v_o1 = mark("sv", V.tensor_scalar(T.O2[K:K + 1, 0:CAP], T.iq[K:K + 1, 0:CAP], float(BLK), float(-BIG), A_.mult, A_.add))
    v_m4 = mark("sv", V.tensor_scalar(T.mask4[0:K, :], T.iq[0:K, 0:4], col("aF"), None, A_.is_equal))
    v_sel = mark("sv", V.tensor_scalar(T.Sel[0:K, :], T.iq[0:K, :], col("bF"), None, A_.is_equal))
    v_lk = mark("sv", V.tensor_scalar(T.l2[K:K + 1, :], T.iq[K:K + 1, :], float(T0), None, A_.add))

    need("v", h_pos)
    c_d = mark("sv", V.tensor_scalar(col("dI"), T.posK[0:K, 0:1], 11, None, A_.logical_shift_right))
    need("v", c_d)
    c_df = mark("sv", V.tensor_copy(col("dF"), col("dI")))
    need("v", c_df)
    c_o = mark("sv", V.tensor_scalar(T.O2[0:K, :], T.iq[0:K, 0:2 * CAP], col("dF"), None, A_.is_equal))
    c_lp = mark("sv", V.tensor_scalar(col("lpI"), T.posK[0:K, 0:1], R - 1, None, A_.bitwise_and))
    need("v", c_lp)
    c_lt = mark("sv", V.tensor_scalar(col("lpT"), col("lpI"), float(-T0), None, A_.add))
    need("a", c_o, v_jf)
    a_r2 = mark("sa", A.activation(T.RP[0:K, N:NL], T.O2[0:K, qp[0]:qp[0] + 2], Copy, scale=col("jF")))
    need("p", c_o, v_or, v_o1, g_l2)
    p_c = mark("sp", P.matmul(T.psC[0:K, 0:2 * CAP], T.LI[0:K + 1, 0:K], T.O2[0:K + 1, 0:2 * CAP], True, True))
    need("v", p_c)
    c_s = mark("sv", V.tensor_reduce(col("slot"), T.psC[0:K, 0:N], X, A_.max))
    c_r = mark("sv", V.tensor_reduce(col("rnk"), T.psC[0:K, CAP:CAP + N], X, A_.max))
    need("a", c_s, v_m4)
    a_ra = mark("sa", A.activation(T.rhsA[0:K, :], T.mask4[0:K, :], Copy, scale=col("slot")))
    need("p", a_ra, v_sel)
    p_a = mark("sp", P.matmul(T.psA[:, 0:4], T.Sel[0:K, :], T.rhsA[0:K, :], True, True))
    need("v", c_r)
    c_l2 = mark("sv", V.tensor_scalar(T.l2[0:K, :], T.iq[0:K, :], col("rnk"), None, A_.is_equal))
    need("a", c_r, c_lt)
    a_w = mark("sa", A.activation(col("w"), col("rnk"), Ident, bias=col("lpT"), scale=-1.0))
    need("a", a_w)
    a_rp = mark("sa", A.activation(T.RP[0:K, 0:N], T.O2[0:K, 0:N], Copy, scale=col("w")))
    need("p", c_l2, a_rp, a_r2, v_rk, v_lk)
    p_b = mark("sp", P.matmul(T.psB[:, 0:NL], T.l2[0:K + 1, :], T.RP[0:K + 1, :], True, True))
    need("a", p_b)
    a_ls = mark("sa", A.activation(T.lst[:, :], T.psB[:, 0:NL], Copy))
    need("v", p_a)
    c_of = mark("sv", V.tensor_copy(T.offS[:, :], T.psA[:, 0:4]))
    need("v", c_of, h_new, v_cm)
    c_sc = mark("sv", V.tensor_copy(T.cmp[:, :].indirect(T.offS[:, 0:4]), T.newS[:, :]))
    need("v", c_sc, a_ls)
    c_pd = mark("sv", V.tensor_copy(T.cmp[:, CAP::BLK], T.lst[:, 0:N]))

    need("g", a_ls)
    g.remote_dma(T.hl[:, :], T.lst[:, :], sem.hin, sem.hsent, pidp, ridp, mp)
    nh = np1
    need("g", c_pd)
    for k in sorted(set(call for (h, q, call, first, n1, n2) in relay if call != PICK)):
        tr = []
        for (h, q, call, first, n1, n2) in relay:
            if call != k:
                continue
            rid, pid = topo.addr(h, core)
            w = BLK * len(q)
            tr.append(RemoteDMATransfer(dst_ids=[DstId(rid=rid, pnc=pid)],
                                        dma_engine_mask=_engines(topo.mask(core, h), first, n1), remote_sem=sem.hin,
                                        src=T.cmp[:, BLK * q[0]:BLK * q[0] + w], dst=T.hbuf[:, 0:w]))
            nh += n1
        g.remote_dma_fused(tr, local_sem=sem.hsent)
    h_sent = ("hsent", nh)
    nd = 0
    for call in calls:
        tr = []
        for (d, first, n) in call:
            rid, pid = topo.addr(cores[d], core)
            tr.append(RemoteDMATransfer(dst_ids=[DstId(rid=rid, pnc=pid)],
                                        dma_engine_mask=_engines(topo.mask(core, cores[d]), first, n), remote_sem=sem.arrD,
                                        src=T.cmp[:, BLK * d:BLK * d + BLK], dst=T.land[:, _slot(d, s, T, topo), :]))
            nd += n
        g.remote_dma_fused(tr, local_sem=sem.dsent)
    h_dsent = ("dsent", nd)

    need("s", c_pd)
    h_own = mark("s_own", S.dma_start(T.land[:, _slot(s, s, T, topo), :], T.cmp[:, BLK * s:BLK * s + BLK]), 16)

    early, late = _order(s, T, topo)
    n_d = sum(n for x in early if x != s for call in _routes(x, T, topo)[1] for (d, first, n) in call if d == s)
    n_x = sum(n2 for x in late for (h, q, call, first, n1, n2) in _routes(x, T, topo)[2] if s in q)
    h_arrD, h_arrX = ("arrD", n_d), ("arrX", n_x)

    def absorb(a, b, o, landed, before):
        need("a", *landed)
        cd = mark("sa", A.activation(T.dat[:, CAP * a:CAP * b], T.land[:, a:b, 0:CAP], Copy))
        need("v", *landed)
        cp = mark("sv", V.tensor_copy(T.offR[:, o:o + b - a], T.land[:, a:b, CAP]))
        need("v", cp, cd, before)
        return mark("sv", V.tensor_copy(T.tabS[:, :].indirect(T.offR[:, o:o + b - a]), T.dat[:, CAP * a:CAP * b]))

    ne = len(early)
    last = absorb(0, ne, 0, (h_own, h_arrD), h_t0)
    last = absorb(ne, N, ne + ne % 2, (h_arrX,), last)
    need("s", last)
    h_st = mark("s_st", S.dma_start(T.y[:, :], T.tabS[:, 0:R]), 16)

    need("g", h_sent, h_dsent, h_rsent, h_st, h_pos, h_new, h_t0, h_own, h_arrD, h_arrX)
    for name in ("sv", "sa", "sp", "sg"):
        need("g", (name, cnt[name]))
